import numpy as np
import ml_dtypes


def mxq(x, axis, fmt="e4m3"):
    dtype, down = {"e4m3": (ml_dtypes.float8_e4m3fn, 7), "e5m2": (ml_dtypes.float8_e5m2, 14)}[fmt]
    v = np.moveaxis(np.asarray(x, np.float32).astype(ml_dtypes.bfloat16).astype(np.float64), axis, -1)
    blocks = v.reshape(v.shape[:-1] + (-1, 32))
    amax = np.abs(blocks).max(-1, keepdims=True)
    byte = np.maximum(np.where(amax > 0, np.frexp(amax)[1] - 1 + 127, 0) - down, 1)
    scale = np.exp2(byte - 127.0)
    codes = (blocks / scale).astype(np.float32).astype(dtype).astype(np.float64)
    return np.moveaxis((codes * scale).reshape(v.shape), -1, axis)


WIDE = False


def mx_kscale(k):
    if not WIDE:
        return np.ones(k)
    levels = np.array([10, -10, 5, -5, 0])
    if k % 512:
        return np.exp2(np.random.permutation(np.resize(levels, k // 32))).repeat(32)
    a = np.empty((k // 512, 16))
    for p in range(k // 512):
        a[p, :8] = np.random.permutation(np.resize(levels, 8))
        for g in range(8):
            far = levels[np.abs(levels - a[p, g]) >= 10]
            a[p, g + 8] = far[np.random.randint(len(far))]
    return np.exp2(a.ravel()).repeat(32)


BF16 = ml_dtypes.bfloat16


def bf(x):
    return np.asarray(x, np.float32).astype(BF16)


def f64(x):
    return np.asarray(x).astype(np.float64)


E2M1 = np.array([0.0, 0.5, 1.0, 1.5, 2.0, 3.0, 4.0, 6.0, -0.0, -0.5, -1.0, -1.5, -2.0, -3.0, -4.0, -6.0])


def pack_weight(w, fmt):
    k, n = w.shape
    w = f64(bf(w)).reshape(k // 32, 32, n)
    amax = np.abs(w).max(1)
    if fmt == "e4m3":
        byte = np.frexp(amax)[1] - 1 + 127 - 7
    else:
        mant, ex = np.frexp(amax / 6.0)
        byte = np.where(mant > 0.5, ex, ex - 1) + 127
    byte = np.clip(np.where(amax > 0, byte, 1), 1, 254)
    scaled = (w * np.exp2(127.0 - byte)[:, None, :]).reshape(k, n).astype(np.float32)
    by_word = np.ascontiguousarray(scaled.reshape(k // 512, 128, 4, n).transpose(0, 1, 3, 2))
    if fmt == "e4m3":
        words = by_word.astype(ml_dtypes.float8_e4m3fn).view(np.uint8)
    else:
        c = by_word.astype(ml_dtypes.float4_e2m1fn).view(np.uint8) & 0xF
        words = c[..., 0::2] | (c[..., 1::2] << 4)
    return np.ascontiguousarray(words), np.ascontiguousarray(byte.astype(np.uint8).reshape(k // 512, 16, n))


def unpack_weight(words, scales, fmt):
    g, p, n, _ = words.shape
    if fmt == "e4m3":
        vals = np.ascontiguousarray(words).view(ml_dtypes.float8_e4m3fn).astype(np.float64)
    else:
        nib = np.empty((g, p, n, 4), np.uint8)
        nib[..., 0::2] = words & 0xF
        nib[..., 1::2] = words >> 4
        vals = E2M1[nib]
    vals = vals * np.repeat(np.exp2(scales.astype(np.float64) - 127.0), 8, axis=1)[..., None]
    return vals.transpose(0, 1, 3, 2).reshape(g * 512, n)
def pack4(w):
    words, scales = pack_weight(w, "e2m1")
    return words.reshape(words.shape[0], 128, -1), scales


def unpack4(words, scales):
    return unpack_weight(words.reshape(words.shape[0], 128, -1, 2), scales, "e2m1")


O, D, KL, KC, S = 1024, 1024, 1024, 3072, 3

STRENGTH = 0.5
LOW, SPAN = 0.2, 1.6


def setup_inputs():
    a, c = mx_kscale(KL), mx_kscale(KC)
    catalogue = STRENGTH * np.random.standard_normal((KC, D)) / np.sqrt(KC) / c[:, None]
    words, scales = pack4(catalogue)
    return {"live": bf(np.random.standard_normal((O, KL)) * a),
            "dest_live": bf(STRENGTH * np.random.standard_normal((KL, D)) / np.sqrt(KL) / a[:, None]),
            "base": bf(np.random.standard_normal((O, KC)) * c),
            "catalogue_words": words,
            "catalogue_scales": scales,
            "log_out": bf(0.3 * np.random.standard_normal(O)),
            "log_in": bf(0.3 * np.random.standard_normal(D)),
            "prevalence": bf(LOW + SPAN * np.random.random((S, O)))}


def reference(live, dest_live, base, catalogue_words, catalogue_scales, log_out, log_in, prevalence):
    travel = mxq(f64(live), 1, "e4m3") @ mxq(f64(dest_live), 0, "e4m3")
    w = unpack4(catalogue_words, catalogue_scales)
    static = mxq(f64(base), 1, "e4m3") @ w
    score = travel + static + f64(log_out)[:, None] + f64(log_in)
    flow = np.exp(score)
    return f64(prevalence)[:, :, None] * flow

@@ -1,0 +1,380 @@
+from contextlib import ExitStack
+
+import concourse.mybir as mybir
+from concourse.masks import make_identity
+
+O, D, KL, KC, S = 1024, 1024, 1024, 3072, 3
+FLOPS = 2 * O * D * (KL + KC)
+
+F32 = mybir.dt.float32
+BF16 = mybir.dt.bfloat16
+I32 = mybir.dt.int32
+U32 = mybir.dt.uint32
+U8 = mybir.dt.uint8
+FP8X4 = mybir.dt.float8_e4m3fn_x4
+FP4X4 = mybir.dt.float4_e2m1fn_x4
+ACT = mybir.ActivationFunctionType
+ALU = mybir.AluOpType
+
+P = 128
+NT = 512
+RT = O // P
+BP = KC // 512
+LP = KL // 512
+PASSES = BP + LP
+
+
+def tile_gravity_importation_scenarios_s1_kernel(
+    tc, live, dest_live, base, catalogue_words, catalogue_scales, log_out, log_in, prevalence, out
+):
+    nc = tc.nc
+    with ExitStack() as ctx:
+        keep = ctx.enter_context(tc.tile_pool(name="keep", bufs=1))
+        rawp = ctx.enter_context(tc.tile_pool(name="rawp", bufs=RT))
+        work = ctx.enter_context(tc.tile_pool(name="work", bufs=2))
+        outp = ctx.enter_context(tc.tile_pool(name="outp", bufs=4))
+        psum = ctx.enter_context(tc.psum_pool(name="psum", bufs=4))
+        ctx.enter_context(tc.manual_schedule())
+
+        ident = keep.tile([P, P], F32, name="ident", align_bytes=64)
+        w_words = keep.tile([P, BP, 2 * D], U8, name="w_words", align_bytes=64)
+        w_scales = keep.tile([P, BP, D], U8, name="w_scales", align_bytes=64)
+        d_raw = [
+            [keep.tile([P, 4, NT], BF16, name=f"d_raw{g}{n}", align_bytes=64) for n in range(2)] for g in range(LP)
+        ]
+        d_codes = keep.tile([P, LP, D], U32, name="d_codes", align_bytes=64)
+        d_scales = keep.tile([P, LP, D], U8, name="d_scales", align_bytes=64)
+        login = keep.tile([P, D], F32, name="login", align_bytes=64)
+        vec_bf = keep.tile([P, P], BF16, name="vec_bf", align_bytes=64)
+        vec_f32 = keep.tile([P, P], F32, name="vec_f32", align_bytes=64)
+        cols = keep.tile([P, 5 * RT], F32, name="cols", align_bytes=64)
+        junk = keep.tile([P, 8], F32, name="junk", align_bytes=64)
+        raw = [rawp.tile([P, KC + KL], BF16, name="raw", tag="raw", align_bytes=64) for r in range(RT)]
+
+        nc.vector.memset(vec_bf[:], 0.0)
+        nc.vector.memset(junk[:], 0.0)
+        make_identity(nc, ident[:])
+        nc.scalar.dma_start(out=vec_bf[0:RT, :], in_=log_out.rearrange("(r p) -> r p", p=P))
+        nc.scalar.dma_start(out=vec_bf[RT : 4 * RT, :], in_=prevalence.rearrange("z (r p) -> (z r) p", p=P))
+        nc.scalar.dma_start(out=vec_bf[4 * RT : 5 * RT, :], in_=log_in.rearrange("(r p) -> r p", p=P))
+        nc.scalar.activation(out=junk[:, 0:1], in_=junk[:, 1:2], func=ACT.Exp)
+        nc.vector.memset(w_scales[:].rearrange("p g n -> p (g n)").bitcast(I32), 0)
+
+        words_src = catalogue_words.bitcast(I32).rearrange("g p n -> p g n")
+        words_dst = w_words[:].rearrange("p g n -> p (g n)").bitcast(I32).rearrange("p (g n) -> p g n", g=BP)
+        scales_src = catalogue_scales.bitcast(I32)
+        scales_dst = w_scales[:].rearrange("p g n -> p (g n)").bitcast(I32).rearrange("p (g n) -> p g n", g=BP)
+        dest_src = dest_live.rearrange("(g p j) n -> g p j n", g=LP, j=4)
+
+        def load_base(r, a, b):
+            nc.sync.dma_start(out=raw[r][:, a:b], in_=base[r * P : (r + 1) * P, a:b])
+
+        def load_live(r):
+            nc.sync.dma_start(out=raw[r][:, KC:], in_=live[r * P : (r + 1) * P, :])
+
+        def load_words(g):
+            nc.sync.dma_start(out=words_dst[:, g : g + 2, :], in_=words_src[:, g : g + 2, :])
+
+        def load_dest(g, n):
+            nc.sync.dma_start(out=d_raw[g][n][:], in_=dest_src[g][:, :, n * NT : (n + 1) * NT])
+
+        load_base(0, 0, 1024)
+        load_base(0, 1024, KC)
+        load_words(0)
+        for q in range(4):
+            nc.sync.dma_start(
+                out=scales_dst[q : P : 32, :, :], in_=scales_src[:, q : 16 : 4, :].rearrange("g r n -> r g n")
+            )
+        load_words(2)
+        load_base(1, 0, KC)
+        load_words(4)
+        load_live(0)
+        load_live(1)
+        for g in range(LP):
+            load_dest(g, 0)
+        load_base(2, 0, KC)
+        load_live(2)
+        for g in range(LP):
+            load_dest(g, 1)
+        for r in range(3, RT):
+            load_base(r, 0, KC)
+            load_live(r)
+
+        perm, grp, codes, scales, tbank, acc, score, flow, res = {}, {}, {}, {}, {}, {}, {}, {}, {}
+
+        def permute(r, a, b):
+            if r not in perm:
+                perm[r] = work.tile([P, (KC + KL) // 2], F32, name="perm", tag="perm", align_bytes=64)
+            nc.vector.tensor_copy(
+                out=perm[r][:, 256 * a : 256 * b].rearrange("q (g u p) -> q g u p", u=2, p=P),
+                in_=raw[r][:].bitcast(F32)[:, 256 * a : 256 * b].rearrange("q (g p u) -> q g u p", u=2, p=P),
+            )
+
+        def turn(r, q, direct=False):
+            bank = psum.tile([P, 2, 2, P], F32, name="tbank", tag="tbank")
+            tbank[r, q] = bank
+            for a in range(2):
+                g = 2 * q + a
+                for u in range(2):
+                    if direct:
+                        src = raw[r][:].bitcast(F32)[:, 256 * g + u : 256 * (g + 1) : 2]
+                    else:
+                        src = perm[r][:, 256 * g + P * u : 256 * g + P * (u + 1)]
+                    nc.tensor.transpose(bank[:, a, u, :], src, ident[:])
+
+        def evac(r, q, on_scalar=True):
+            if r not in grp:
+                grp[r] = work.tile([P, PASSES * 512], BF16, name="grp", tag="grp", align_bytes=64)
+            dst = grp[r][:, 1024 * q : 1024 * (q + 1)].bitcast(F32).rearrange("p (a r u) -> p a r u", a=2, u=2)
+            src = tbank[r, q][:].rearrange("p a u r -> p a r u")
+            if on_scalar:
+                nc.scalar.copy(out=dst, in_=src)
+            else:
+                nc.vector.tensor_copy(out=dst, in_=src)
+
+        def quant(r, a, b):
+            if r not in codes:
+                codes[r] = work.tile([P, PASSES * P], U32, name="codes", tag="codes", bufs=3, align_bytes=64)
+                scales[r] = work.tile([P, PASSES * P], U8, name="scales", tag="scales", bufs=3, align_bytes=64)
+            nc.vector.quantize_mx(
+                out=codes[r][:, 256 * a : 256 * b].bitcast(FP8X4),
+                scales=scales[r][:, 256 * a : 256 * b],
+                in_=grp[r][:, 1024 * a : 1024 * b],
+            )
+
+        d_grp = {}
+
+        def interleave(g, n, half, on_scalar):
+            if (g, n) not in d_grp:
+                d_grp[g, n] = work.tile([P, NT, 4], BF16, name="d_grp", tag="d_grp", align_bytes=64)
+            part = slice(half * NT // 2, (half + 1) * NT // 2)
+            dst = d_grp[g, n][:, part, :]
+            src = d_raw[g][n][:, :, part].rearrange("p j n -> p n j")
+            if on_scalar:
+                nc.scalar.copy(out=dst, in_=src)
+            else:
+                nc.vector.tensor_copy(out=dst, in_=src)
+
+        def quant_dest(g, n):
+            nc.vector.quantize_mx(
+                out=d_codes[:, g, n * NT : (n + 1) * NT].bitcast(FP8X4),
+                scales=d_scales[:, g, n * NT : (n + 1) * NT],
+                in_=d_grp[g, n][:].rearrange("p n j -> p (n j)"),
+            )
+
+        def mm(r, n, g):
+            if g == 0:
+                acc[r, n] = psum.tile([P, NT], F32, name="acc", tag="acc")
+            if g < BP:
+                rhs = w_words[:, g, 2 * n * NT : 2 * (n + 1) * NT].bitcast(FP4X4)
+                rhs_scale = w_scales[:, g, n * NT : (n + 1) * NT]
+            else:
+                rhs = d_codes[:, g - BP, n * NT : (n + 1) * NT].bitcast(FP8X4)
+                rhs_scale = d_scales[:, g - BP, n * NT : (n + 1) * NT]
+            nc.tensor.matmul_mx(
+                out=acc[r, n][:],
+                lhsT=codes[r][:, g * P : (g + 1) * P].bitcast(FP8X4),
+                lhsT_scale=scales[r][:, g * P : (g + 1) * P],
+                rhs=rhs,
+                rhs_scale=rhs_scale,
+                start=(g == 0),
+                stop=(g == PASSES - 1),
+            )
+
+        def add(r, n):
+            score[r, n] = work.tile([P, NT], F32, name="score", tag="score", bufs=4, align_bytes=64)
+            nc.vector.tensor_tensor(
+                out=score[r, n][:], in0=acc[r, n][:], in1=login[:, n * NT : (n + 1) * NT], op=ALU.add
+            )
+
+        def exp(r, n):
+            flow[r, n] = work.tile([P, NT], F32, name="flow", tag="flow", bufs=4, align_bytes=64)
+            nc.scalar.activation(out=flow[r, n][:], in_=score[r, n][:], func=ACT.Exp, bias=cols[:, r : r + 1])
+
+        def mul(r, n, z):
+            if (r, z) not in res:
+                res[r, z] = outp.tile([P, D], F32, name=f"res{z}", tag=f"res{z}", align_bytes=64)
+            dst = res[r, z][:, n * NT : (n + 1) * NT]
+            col = cols[:, (z + 1) * RT + r : (z + 1) * RT + r + 1]
+            if z == 2:
+                nc.scalar.activation(out=dst, in_=flow[r, n][:], func=ACT.Copy, scale=col)
+            else:
+                nc.vector.tensor_scalar(out=dst, in0=flow[r, n][:], scalar1=col, scalar2=None, op0=ALU.mult)
+
+        def store(r, z):
+            nc.sync.dma_start(out=out[z, r * P : (r + 1) * P, :], in_=res[r, z][:])
+
+        def store_half(r, n, z):
+            nc.sync.dma_start(
+                out=out[z, r * P : (r + 1) * P, n * NT : (n + 1) * NT], in_=res[r, z][:, n * NT : (n + 1) * NT]
+            )
+
+        def mul_v(r, n):
+            mul(r, n, 0)
+            mul(r, n, 1)
+
+        for q in range(3):
+            turn(0, q, direct=True)
+        nc.vector.tensor_copy(out=vec_f32[:], in_=vec_bf[:])
+        vec_bank = psum.tile([P, 2, 2, P], F32, name="vec_bank", tag="tbank")
+        nc.tensor.transpose(vec_bank[:, 0, 0, :], vec_f32[:], ident[:])
+        evac(0, 0)
+        evac(0, 1, on_scalar=False)
+        evac(0, 2)
+        for q in range(3):
+            quant(0, q, q + 1)
+        nc.vector.tensor_copy(out=cols[:], in_=vec_bank[:, 0, 0, 0 : 5 * RT])
+        for g in range(BP):
+            for n in range(2):
+                mm(0, n, g)
+        permute(1, 0, BP)
+        permute(0, BP, PASSES)
+        permute(1, BP, PASSES)
+        turn(1, 0)
+        evac(1, 0)
+        turn(1, 1)
+        evac(1, 1, on_scalar=False)
+        turn(1, 2)
+        evac(1, 2)
+        turn(0, 3)
+        quant(1, 0, 1)
+        quant(1, 1, 2)
+        evac(0, 3, on_scalar=False)
+        turn(1, 3)
+        evac(1, 3)
+        quant(1, 2, 3)
+        login_bank = []
+        for n in range(2):
+            bank = psum.tile([P, 4, P], F32, name="login_bank", tag="tbank")
+            login_bank.append(bank)
+            for c in range(4):
+                col = 4 * RT + 4 * n + c
+                nc.tensor.transpose(bank[:, c, :], cols[:, col : col + 1].to_broadcast([P, P]), ident[:])
+        for g in range(BP):
+            for n in range(2):
+                mm(1, n, g)
+
+        def login_copy(n):
+            nc.scalar.copy(out=login[:, n * NT : (n + 1) * NT], in_=login_bank[n][:].rearrange("p c r -> p (c r)"))
+
+        interleave(0, 0, 1, True)
+        interleave(0, 0, 0, False)
+        quant(0, 3, 4)
+        interleave(1, 0, 0, False)
+        quant(1, 3, 4)
+        interleave(1, 0, 1, True)
+        quant_dest(0, 0)
+        login_copy(0)
+        login_copy(1)
+        quant_dest(1, 0)
+        for r in range(2):
+            for g in range(BP, PASSES):
+                mm(r, 0, g)
+        permute(2, 0, PASSES)
+        for q in range(4):
+            turn(2, q)
+        interleave(0, 1, 0, False)
+        interleave(0, 1, 1, True)
+        add(0, 0)
+        interleave(1, 1, 0, False)
+        interleave(1, 1, 1, True)
+        evac(2, 0)
+        evac(2, 1)
+        quant_dest(0, 1)
+        exp(0, 0)
+        quant_dest(1, 1)
+        evac(2, 2)
+        evac(2, 3)
+        for r in range(2):
+            for g in range(BP, PASSES):
+                mm(r, 1, g)
+        add(1, 0)
+        quant(2, 0, 2)
+        exp(1, 0)
+        permute(3, 0, PASSES)
+        quant(2, 2, 4)
+        for g in range(PASSES):
+            mm(2, 0, g)
+        for q in range(4):
+            turn(3, q)
+        for g in range(PASSES):
+            mm(2, 1, g)
+        add(0, 1)
+        exp(0, 1)
+        add(1, 1)
+        mul_v(0, 0)
+        exp(1, 1)
+        mul(0, 0, 2)
+        permute(4, 0, BP)
+        mul_v(0, 1)
+        mul(0, 1, 2)
+        evac(3, 0)
+        evac(3, 1, on_scalar=False)
+        evac(3, 2)
+        quant(3, 0, 2)
+        evac(3, 3)
+        permute(4, BP, PASSES)
+        add(2, 0)
+        quant(3, 2, 4)
+        for z in range(3):
+            store(0, z)
+        mul_v(1, 0)
+        mul(1, 0, 2)
+        exp(2, 0)
+        mul_v(1, 1)
+        mul(1, 1, 2)
+        for z in range(3):
+            store(1, z)
+
+
+        for r in range(3, RT - 1):
+            nxt = r + 1
+            for q in range(4):
+                turn(nxt, q)
+            add(r - 1, 1)
+            for n in range(2):
+                for g in range(PASSES):
+                    mm(r, n, g)
+            evac(nxt, 0)
+            evac(nxt, 1)
+            exp(r - 1, 1)
+            mul_v(r - 1, 0)
+            mul(r - 1, 0, 2)
+            if r + 2 < RT:
+                permute(r + 2, 0, BP)
+            quant(nxt, 0, 2)
+            evac(nxt, 2)
+            evac(nxt, 3)
+            mul_v(r - 1, 1)
+            mul(r - 1, 1, 2)
+            for z in range(3):
+                store(r - 1, z)
+            if r + 2 < RT:
+                permute(r + 2, BP, PASSES)
+            quant(nxt, 2, 4)
+            add(r, 0)
+            exp(r, 0)
+
+        last = RT - 1
+        for n in range(2):
+            for g in range(PASSES):
+                mm(last, n, g)
+        add(last - 1, 1)
+        exp(last - 1, 1)
+        mul_v(last - 1, 0)
+        mul(last - 1, 0, 2)
+        mul_v(last - 1, 1)
+        add(last, 0)
+        exp(last, 0)
+        mul(last - 1, 1, 2)
+        for z in range(3):
+            store(last - 1, z)
+        mul_v(last, 0)
+        mul(last, 0, 2)
+        for z in range(3):
+            store_half(last, 0, z)
+        add(last, 1)
+        exp(last, 1)
+        for z in (0, 2, 1):
+            mul(last, 1, z)
+            store_half(last, 1, z)

@@ -22,6 +22,9 @@ RT = O // P
 BP = KC // 512
 LP = KL // 512
 PASSES = BP + LP
+TURN_BANKS = ((4, 6, 7, 4), (5, 4, 5, 5))
+LAST_CHUNKS = ((0, 256), (256, 512))
+SCALE_PARTS = ((0, 2), (2, BP))
 
 
 def tile_gravity_importation_scenarios_s1_kernel(
@@ -30,15 +33,17 @@ def tile_gravity_importation_scenarios_s1_kernel(
     nc = tc.nc
     with ExitStack() as ctx:
         keep = ctx.enter_context(tc.tile_pool(name="keep", bufs=1))
-        rawp = ctx.enter_context(tc.tile_pool(name="rawp", bufs=RT))
+        rawp = ctx.enter_context(tc.tile_pool(name="rawp", bufs=6))
         work = ctx.enter_context(tc.tile_pool(name="work", bufs=2))
-        outp = ctx.enter_context(tc.tile_pool(name="outp", bufs=4))
-        psum = ctx.enter_context(tc.psum_pool(name="psum", bufs=4))
+        outp = ctx.enter_context(tc.tile_pool(name="outp", bufs=3))
+        psum = ctx.enter_context(tc.psum_pool(name="psum", bufs=1))
         ctx.enter_context(tc.manual_schedule())
 
         ident = keep.tile([P, P], F32, name="ident", align_bytes=64)
         w_words = keep.tile([P, BP, 2 * D], U8, name="w_words", align_bytes=64)
-        w_scales = keep.tile([P, BP, D], U8, name="w_scales", align_bytes=64)
+        w_scales = [
+            keep.tile([P, b - a, D], U8, name=f"w_scales{a}", align_bytes=64) for a, b in SCALE_PARTS
+        ]
         d_raw = [
             [keep.tile([P, 4, NT], BF16, name=f"d_raw{g}{n}", align_bytes=64) for n in range(2)] for g in range(LP)
         ]
@@ -49,24 +54,29 @@ def tile_gravity_importation_scenarios_s1_kernel(
         vec_f32 = keep.tile([P, P], F32, name="vec_f32", align_bytes=64)
         cols = keep.tile([P, 5 * RT], F32, name="cols", align_bytes=64)
         junk = keep.tile([P, 8], F32, name="junk", align_bytes=64)
-        raw = [rawp.tile([P, KC + KL], BF16, name="raw", tag="raw", align_bytes=64) for r in range(RT)]
+        raw = {}
 
+        for part in w_scales:
+            nc.vector.memset(part[:].rearrange("p g n -> p (g n)").bitcast(I32), 0)
         nc.vector.memset(vec_bf[:], 0.0)
         nc.vector.memset(junk[:], 0.0)
         make_identity(nc, ident[:])
-        nc.scalar.dma_start(out=vec_bf[0:RT, :], in_=log_out.rearrange("(r p) -> r p", p=P))
-        nc.scalar.dma_start(out=vec_bf[RT : 4 * RT, :], in_=prevalence.rearrange("z (r p) -> (z r) p", p=P))
-        nc.scalar.dma_start(out=vec_bf[4 * RT : 5 * RT, :], in_=log_in.rearrange("(r p) -> r p", p=P))
+        scales_src = catalogue_scales.bitcast(I32)
         nc.scalar.activation(out=junk[:, 0:1], in_=junk[:, 1:2], func=ACT.Exp)
-        nc.vector.memset(w_scales[:].rearrange("p g n -> p (g n)").bitcast(I32), 0)
 
         words_src = catalogue_words.bitcast(I32).rearrange("g p n -> p g n")
         words_dst = w_words[:].rearrange("p g n -> p (g n)").bitcast(I32).rearrange("p (g n) -> p g n", g=BP)
-        scales_src = catalogue_scales.bitcast(I32)
-        scales_dst = w_scales[:].rearrange("p g n -> p (g n)").bitcast(I32).rearrange("p (g n) -> p g n", g=BP)
         dest_src = dest_live.rearrange("(g p j) n -> g p j n", g=LP, j=4)
 
+        def load_scales(i):
+            a, b = SCALE_PARTS[i]
+            dst = w_scales[i][:].rearrange("p g n -> p (g n)").bitcast(I32).rearrange("p (g n) -> p g n", g=b - a)
+            for q in range(4):
+                nc.sync.dma_start(out=dst[q : P : 32, :, :], in_=scales_src[a:b, q : 16 : 4, :].rearrange("g r n -> r g n"))
+
         def load_base(r, a, b):
+            if r not in raw:
+                raw[r] = rawp.tile([P, KC + KL], BF16, name="raw", tag="raw", align_bytes=64)
             nc.sync.dma_start(out=raw[r][:, a:b], in_=base[r * P : (r + 1) * P, a:b])
 
         def load_live(r):
@@ -79,14 +89,16 @@ def tile_gravity_importation_scenarios_s1_kernel(
             nc.sync.dma_start(out=d_raw[g][n][:], in_=dest_src[g][:, :, n * NT : (n + 1) * NT])
 
         load_base(0, 0, 1024)
-        load_base(0, 1024, KC)
+        load_scales(0)
         load_words(0)
-        for q in range(4):
-            nc.sync.dma_start(
-                out=scales_dst[q : P : 32, :, :], in_=scales_src[:, q : 16 : 4, :].rearrange("g r n -> r g n")
-            )
+        load_base(1, 0, 1024)
+        load_base(0, 1024, KC)
+        load_scales(1)
         load_words(2)
-        load_base(1, 0, KC)
+        load_base(1, 1024, KC)
+        nc.sync.dma_start(out=vec_bf[0:RT, :], in_=log_out.rearrange("(r p) -> r p", p=P))
+        nc.sync.dma_start(out=vec_bf[RT : 4 * RT, :], in_=prevalence.rearrange("z (r p) -> (z r) p", p=P))
+        nc.sync.dma_start(out=vec_bf[4 * RT : 5 * RT, :], in_=log_in.rearrange("(r p) -> r p", p=P))
         load_words(4)
         load_live(0)
         load_live(1)
@@ -96,7 +108,7 @@ def tile_gravity_importation_scenarios_s1_kernel(
         load_live(2)
         for g in range(LP):
             load_dest(g, 1)
-        for r in range(3, RT):
+        for r in range(3, 6):
             load_base(r, 0, KC)
             load_live(r)
 
@@ -104,14 +116,15 @@ def tile_gravity_importation_scenarios_s1_kernel(
 
         def permute(r, a, b):
             if r not in perm:
-                perm[r] = work.tile([P, (KC + KL) // 2], F32, name="perm", tag="perm", align_bytes=64)
+                perm[r] = work.tile([P, (KC + KL) // 2], F32, name="perm", tag="perm", bufs=3, align_bytes=64)
             nc.vector.tensor_copy(
                 out=perm[r][:, 256 * a : 256 * b].rearrange("q (g u p) -> q g u p", u=2, p=P),
                 in_=raw[r][:].bitcast(F32)[:, 256 * a : 256 * b].rearrange("q (g p u) -> q g u p", u=2, p=P),
             )
 
         def turn(r, q, direct=False):
-            bank = psum.tile([P, 2, 2, P], F32, name="tbank", tag="tbank")
+            b = 4 + q if r > 1 else TURN_BANKS[r][q]
+            bank = psum.tile([P, 2, 2, P], F32, name="tbank", tag=f"bank{b}")
             tbank[r, q] = bank
             for a in range(2):
                 g = 2 * q + a
@@ -124,7 +137,7 @@ def tile_gravity_importation_scenarios_s1_kernel(
 
         def evac(r, q, on_scalar=True):
             if r not in grp:
-                grp[r] = work.tile([P, PASSES * 512], BF16, name="grp", tag="grp", align_bytes=64)
+                grp[r] = work.tile([P, PASSES * 512], BF16, name="grp", tag="grp", bufs=3, align_bytes=64)
             dst = grp[r][:, 1024 * q : 1024 * (q + 1)].bitcast(F32).rearrange("p (a r u) -> p a r u", a=2, u=2)
             src = tbank[r, q][:].rearrange("p a u r -> p a r u")
             if on_scalar:
@@ -134,8 +147,8 @@ def tile_gravity_importation_scenarios_s1_kernel(
 
         def quant(r, a, b):
             if r not in codes:
-                codes[r] = work.tile([P, PASSES * P], U32, name="codes", tag="codes", bufs=3, align_bytes=64)
-                scales[r] = work.tile([P, PASSES * P], U8, name="scales", tag="scales", bufs=3, align_bytes=64)
+                codes[r] = work.tile([P, PASSES * P], U32, name="codes", tag="codes", bufs=4, align_bytes=64)
+                scales[r] = work.tile([P, PASSES * P], U8, name="scales", tag="scales", bufs=4, align_bytes=64)
             nc.vector.quantize_mx(
                 out=codes[r][:, 256 * a : 256 * b].bitcast(FP8X4),
                 scales=scales[r][:, 256 * a : 256 * b],
@@ -162,15 +175,18 @@ def tile_gravity_importation_scenarios_s1_kernel(
                 in_=d_grp[g, n][:].rearrange("p n j -> p (n j)"),
             )
 
+        def moving(g, lo, width):
+            if g < BP:
+                i = 0 if g < SCALE_PARTS[0][1] else 1
+                words = w_words[:, g, 2 * lo : 2 * (lo + width)].bitcast(FP4X4)
+                return words, w_scales[i][:, g - SCALE_PARTS[i][0], lo : lo + width]
+            return d_codes[:, g - BP, lo : lo + width].bitcast(FP8X4), d_scales[:, g - BP, lo : lo + width]
+
         def mm(r, n, g):
             if g == 0:
-                acc[r, n] = psum.tile([P, NT], F32, name="acc", tag="acc")
-            if g < BP:
-                rhs = w_words[:, g, 2 * n * NT : 2 * (n + 1) * NT].bitcast(FP4X4)
-                rhs_scale = w_scales[:, g, n * NT : (n + 1) * NT]
-            else:
-                rhs = d_codes[:, g - BP, n * NT : (n + 1) * NT].bitcast(FP8X4)
-                rhs_scale = d_scales[:, g - BP, n * NT : (n + 1) * NT]
+                b = 2 * (r % 2) + n
+                acc[r, n] = psum.tile([P, NT], F32, name="acc", tag=f"bank{b}")
+            rhs, rhs_scale = moving(g, n * NT, NT)
             nc.tensor.matmul_mx(
                 out=acc[r, n][:],
                 lhsT=codes[r][:, g * P : (g + 1) * P].bitcast(FP8X4),
@@ -213,119 +229,128 @@ def tile_gravity_importation_scenarios_s1_kernel(
             mul(r, n, 0)
             mul(r, n, 1)
 
-        for q in range(3):
-            turn(0, q, direct=True)
-        nc.vector.tensor_copy(out=vec_f32[:], in_=vec_bf[:])
-        vec_bank = psum.tile([P, 2, 2, P], F32, name="vec_bank", tag="tbank")
-        nc.tensor.transpose(vec_bank[:, 0, 0, :], vec_f32[:], ident[:])
+        def mm_part(r, c):
+            for g in (2 * c, 2 * c + 1):
+                for n in range(2):
+                    mm(r, n, g)
+
+        def mm_live(n):
+            for r in range(2):
+                for g in range(BP, PASSES):
+                    mm(r, n, g)
+
+        turn(0, 0, direct=True)
         evac(0, 0)
-        evac(0, 1, on_scalar=False)
-        evac(0, 2)
-        for q in range(3):
-            quant(0, q, q + 1)
-        nc.vector.tensor_copy(out=cols[:], in_=vec_bank[:, 0, 0, 0 : 5 * RT])
-        for g in range(BP):
-            for n in range(2):
-                mm(0, n, g)
-        permute(1, 0, BP)
+        turn(1, 0, direct=True)
+        evac(1, 0)
+        quant(0, 0, 1)
+        mm_part(0, 0)
+        permute(0, 2, BP)
+        quant(1, 0, 1)
+        turn(0, 1)
+        turn(0, 2)
+        mm_part(1, 0)
+        permute(1, 2, BP)
+        evac(0, 1)
+        evac(0, 2, on_scalar=False)
+        quant(0, 1, 2)
+        quant(0, 2, 3)
+        nc.vector.tensor_copy(out=vec_f32[:], in_=vec_bf[:])
         permute(0, BP, PASSES)
         permute(1, BP, PASSES)
-        turn(1, 0)
-        evac(1, 0)
         turn(1, 1)
-        evac(1, 1, on_scalar=False)
         turn(1, 2)
-        evac(1, 2)
-        turn(0, 3)
-        quant(1, 0, 1)
+        vec_bank = psum.tile([P, 2, 2, P], F32, name="vec_bank", tag="bank6")
+        nc.tensor.transpose(vec_bank[:, 0, 0, :], vec_f32[:], ident[:])
+        mm_part(0, 1)
+        mm_part(0, 2)
+        evac(1, 1)
+        evac(1, 2, on_scalar=False)
+        nc.scalar.copy(out=cols[:], in_=vec_bank[:, 0, 0, 0 : 5 * RT])
         quant(1, 1, 2)
-        evac(0, 3, on_scalar=False)
-        turn(1, 3)
-        evac(1, 3)
+        interleave(0, 0, 0, True)
+        interleave(0, 0, 1, False)
+        interleave(1, 0, 0, True)
+        interleave(1, 0, 1, False)
         quant(1, 2, 3)
+        quant_dest(0, 0)
+        for r in range(6, RT):
+            load_base(r, 0, KC)
+            load_live(r)
+        turn(0, 3)
+        turn(1, 3)
         login_bank = []
         for n in range(2):
-            bank = psum.tile([P, 4, P], F32, name="login_bank", tag="tbank")
+            bank = psum.tile([P, 4, P], F32, name="login_bank", tag=f"bank{6 + n}")
             login_bank.append(bank)
             for c in range(4):
                 col = 4 * RT + 4 * n + c
                 nc.tensor.transpose(bank[:, c, :], cols[:, col : col + 1].to_broadcast([P, P]), ident[:])
-        for g in range(BP):
-            for n in range(2):
-                mm(1, n, g)
-
-        def login_copy(n):
+        mm_part(1, 1)
+        mm_part(1, 2)
+        evac(0, 3)
+        evac(1, 3, on_scalar=False)
+        for n in range(2):
             nc.scalar.copy(out=login[:, n * NT : (n + 1) * NT], in_=login_bank[n][:].rearrange("p c r -> p (c r)"))
-
-        interleave(0, 0, 1, True)
-        interleave(0, 0, 0, False)
         quant(0, 3, 4)
-        interleave(1, 0, 0, False)
-        quant(1, 3, 4)
-        interleave(1, 0, 1, True)
-        quant_dest(0, 0)
-        login_copy(0)
-        login_copy(1)
         quant_dest(1, 0)
-        for r in range(2):
-            for g in range(BP, PASSES):
-                mm(r, 0, g)
-        permute(2, 0, PASSES)
+        permute(2, 0, BP)
+        quant(1, 3, 4)
+        mm_live(0)
+        interleave(0, 1, 0, True)
+        interleave(0, 1, 1, False)
+        interleave(1, 1, 0, True)
+        interleave(1, 1, 1, False)
+        permute(2, BP, PASSES)
         for q in range(4):
             turn(2, q)
-        interleave(0, 1, 0, False)
-        interleave(0, 1, 1, True)
-        add(0, 0)
-        interleave(1, 1, 0, False)
-        interleave(1, 1, 1, True)
-        evac(2, 0)
-        evac(2, 1)
         quant_dest(0, 1)
-        exp(0, 0)
+        evac(2, 0)
+        add(0, 0)
+        evac(2, 1)
         quant_dest(1, 1)
-        evac(2, 2)
-        evac(2, 3)
-        for r in range(2):
-            for g in range(BP, PASSES):
-                mm(r, 1, g)
+        mm_live(1)
+        exp(0, 0)
         add(1, 0)
+        evac(2, 2)
         quant(2, 0, 2)
         exp(1, 0)
-        permute(3, 0, PASSES)
+        evac(2, 3, on_scalar=False)
+        add(0, 1)
         quant(2, 2, 4)
+        permute(3, 0, PASSES)
+        exp(0, 1)
+        mul(0, 0, 2)
+        add(1, 1)
+        mul_v(0, 0)
+        mul(1, 0, 2)
         for g in range(PASSES):
             mm(2, 0, g)
         for q in range(4):
             turn(3, q)
         for g in range(PASSES):
             mm(2, 1, g)
-        add(0, 1)
-        exp(0, 1)
-        add(1, 1)
-        mul_v(0, 0)
         exp(1, 1)
-        mul(0, 0, 2)
-        permute(4, 0, BP)
-        mul_v(0, 1)
-        mul(0, 1, 2)
         evac(3, 0)
-        evac(3, 1, on_scalar=False)
+        permute(4, 0, PASSES)
+        evac(3, 1)
+        mul(0, 1, 2)
+        add(2, 0)
         evac(3, 2)
         quant(3, 0, 2)
         evac(3, 3)
-        permute(4, BP, PASSES)
-        add(2, 0)
-        quant(3, 2, 4)
+        mul_v(0, 1)
         for z in range(3):
             store(0, z)
-        mul_v(1, 0)
-        mul(1, 0, 2)
         exp(2, 0)
-        mul_v(1, 1)
+        mul_v(1, 0)
+        quant(3, 2, 4)
         mul(1, 1, 2)
+        mul_v(1, 1)
         for z in range(3):
             store(1, z)
-
+        mul(2, 0, 2)
+        mul_v(2, 0)
 
         for r in range(3, RT - 1):
             nxt = r + 1
@@ -336,45 +361,88 @@ def tile_gravity_importation_scenarios_s1_kernel(
                 for g in range(PASSES):
                     mm(r, n, g)
             evac(nxt, 0)
-            evac(nxt, 1)
             exp(r - 1, 1)
-            mul_v(r - 1, 0)
-            mul(r - 1, 0, 2)
+            evac(nxt, 1)
             if r + 2 < RT:
-                permute(r + 2, 0, BP)
-            quant(nxt, 0, 2)
-            evac(nxt, 2)
-            evac(nxt, 3)
+                permute(r + 2, 0, PASSES)
             mul_v(r - 1, 1)
+            evac(nxt, 2)
+            quant(nxt, 0, 2)
             mul(r - 1, 1, 2)
             for z in range(3):
                 store(r - 1, z)
-            if r + 2 < RT:
-                permute(r + 2, BP, PASSES)
-            quant(nxt, 2, 4)
+            evac(nxt, 3)
             add(r, 0)
             exp(r, 0)
+            quant(nxt, 2, 4)
+            mul(r, 0, 2)
+            mul_v(r, 0)
 
         last = RT - 1
-        for n in range(2):
-            for g in range(PASSES):
-                mm(last, n, g)
+        for z in range(3):
+            store_half(last - 1, 0, z)
+        for g in range(PASSES):
+            mm(last, 0, g)
         add(last - 1, 1)
         exp(last - 1, 1)
-        mul_v(last - 1, 0)
-        mul(last - 1, 0, 2)
         mul_v(last - 1, 1)
-        add(last, 0)
-        exp(last, 0)
         mul(last - 1, 1, 2)
         for z in range(3):
-            store(last - 1, z)
+            store_half(last - 1, 1, z)
+        def last_add(i):
+            lo, hi = LAST_CHUNKS[i]
+            bank = psum.tile([P, NT], F32, name="acc", tag=f"bank{3 + i}")
+            for c in range(lo, hi, P):
+                for g in range(PASSES):
+                    rhs, rhs_scale = moving(g, NT + c, P)
+                    nc.tensor.matmul_mx(
+                        out=bank[:, c - lo : c - lo + P],
+                        lhsT=codes[last][:, g * P : (g + 1) * P].bitcast(FP8X4),
+                        lhsT_scale=scales[last][:, g * P : (g + 1) * P],
+                        rhs=rhs,
+                        rhs_scale=rhs_scale,
+                        start=(g == 0),
+                        stop=(g == PASSES - 1),
+                    )
+            score[last, 1 + i] = work.tile([P, NT], F32, name="score", tag="score", bufs=4, align_bytes=64)
+            nc.vector.tensor_tensor(
+                out=score[last, 1 + i][:, : hi - lo],
+                in0=bank[:, : hi - lo],
+                in1=login[:, NT + lo : NT + hi],
+                op=ALU.add,
+            )
+
+        def last_exp(i):
+            w = LAST_CHUNKS[i][1] - LAST_CHUNKS[i][0]
+            flow[last, 1 + i] = work.tile([P, NT], F32, name="flow", tag="flow", bufs=4, align_bytes=64)
+            nc.scalar.activation(
+                out=flow[last, 1 + i][:, :w],
+                in_=score[last, 1 + i][:, :w],
+                func=ACT.Exp,
+                bias=cols[:, last : last + 1],
+            )
+
+        def last_mul(i):
+            lo, hi = LAST_CHUNKS[i]
+            for z in (0, 2, 1):
+                col = cols[:, (z + 1) * RT + last : (z + 1) * RT + last + 1]
+                dst = res[last, z][:, NT + lo : NT + hi]
+                src = flow[last, 1 + i][:, : hi - lo]
+                if z == 2:
+                    nc.scalar.activation(out=dst, in_=src, func=ACT.Copy, scale=col)
+                else:
+                    nc.vector.tensor_scalar(out=dst, in0=src, scalar1=col, scalar2=None, op0=ALU.mult)
+                nc.sync.dma_start(out=out[z, last * P : (last + 1) * P, NT + lo : NT + hi], in_=dst)
+
+        add(last, 0)
+        exp(last, 0)
+        last_add(0)
         mul_v(last, 0)
+        last_exp(0)
         mul(last, 0, 2)
         for z in range(3):
             store_half(last, 0, z)
-        add(last, 1)
-        exp(last, 1)
-        for z in (0, 2, 1):
-            mul(last, 1, z)
-            store_half(last, 1, z)
+        last_add(1)
+        last_exp(1)
+        last_mul(0)
+        last_mul(1)

@@ -22,9 +22,9 @@ RT = O // P
 BP = KC // 512
 LP = KL // 512
 PASSES = BP + LP
+HALVES_FROM = 4
 TURN_BANKS = ((4, 6, 7, 4), (5, 4, 5, 5))
 LAST_CHUNKS = ((0, 256), (256, 512))
-SCALE_PARTS = ((0, 2), (2, BP))
 
 
 def tile_gravity_importation_scenarios_s1_kernel(
@@ -41,9 +41,7 @@ def tile_gravity_importation_scenarios_s1_kernel(
 
         ident = keep.tile([P, P], F32, name="ident", align_bytes=64)
         w_words = keep.tile([P, BP, 2 * D], U8, name="w_words", align_bytes=64)
-        w_scales = [
-            keep.tile([P, b - a, D], U8, name=f"w_scales{a}", align_bytes=64) for a, b in SCALE_PARTS
-        ]
+        w_scales = keep.tile([P, BP, D], U8, name="w_scales", align_bytes=64)
         d_raw = [
             [keep.tile([P, 4, NT], BF16, name=f"d_raw{g}{n}", align_bytes=64) for n in range(2)] for g in range(LP)
         ]
@@ -56,8 +54,9 @@ def tile_gravity_importation_scenarios_s1_kernel(
         junk = keep.tile([P, 8], F32, name="junk", align_bytes=64)
         raw = {}
 
-        for part in w_scales:
-            nc.vector.memset(part[:].rearrange("p g n -> p (g n)").bitcast(I32), 0)
+        scales_flat = w_scales[:].rearrange("p g n -> p (g n)").bitcast(I32)
+        nc.vector.memset(scales_flat[:, 0:1024], 0)
+        nc.gpsimd.memset(scales_flat[:, 1024:], 0)
         nc.vector.memset(vec_bf[:], 0.0)
         nc.vector.memset(junk[:], 0.0)
         make_identity(nc, ident[:])
@@ -68,11 +67,10 @@ def tile_gravity_importation_scenarios_s1_kernel(
         words_dst = w_words[:].rearrange("p g n -> p (g n)").bitcast(I32).rearrange("p (g n) -> p g n", g=BP)
         dest_src = dest_live.rearrange("(g p j) n -> g p j n", g=LP, j=4)
 
-        def load_scales(i):
-            a, b = SCALE_PARTS[i]
-            dst = w_scales[i][:].rearrange("p g n -> p (g n)").bitcast(I32).rearrange("p (g n) -> p g n", g=b - a)
+        def load_scales():
+            dst = scales_flat.rearrange("p (g n) -> p g n", g=BP)
             for q in range(4):
-                nc.sync.dma_start(out=dst[q : P : 32, :, :], in_=scales_src[a:b, q : 16 : 4, :].rearrange("g r n -> r g n"))
+                nc.sync.dma_start(out=dst[q : P : 32, :, :], in_=scales_src[:, q : 16 : 4, :].rearrange("g r n -> r g n"))
 
         def load_base(r, a, b):
             if r not in raw:
@@ -89,19 +87,18 @@ def tile_gravity_importation_scenarios_s1_kernel(
             nc.sync.dma_start(out=d_raw[g][n][:], in_=dest_src[g][:, :, n * NT : (n + 1) * NT])
 
         load_base(0, 0, 1024)
-        load_scales(0)
-        load_words(0)
+        load_scales()
         load_base(1, 0, 1024)
+        load_words(0)
         load_base(0, 1024, KC)
-        load_scales(1)
         load_words(2)
         load_base(1, 1024, KC)
-        nc.sync.dma_start(out=vec_bf[0:RT, :], in_=log_out.rearrange("(r p) -> r p", p=P))
-        nc.sync.dma_start(out=vec_bf[RT : 4 * RT, :], in_=prevalence.rearrange("z (r p) -> (z r) p", p=P))
-        nc.sync.dma_start(out=vec_bf[4 * RT : 5 * RT, :], in_=log_in.rearrange("(r p) -> r p", p=P))
         load_words(4)
         load_live(0)
         load_live(1)
+        nc.gpsimd.dma_start(out=vec_bf[0:RT, :], in_=log_out.rearrange("(r p) -> r p", p=P))
+        nc.gpsimd.dma_start(out=vec_bf[RT : 4 * RT, :], in_=prevalence.rearrange("z (r p) -> (z r) p", p=P))
+        nc.gpsimd.dma_start(out=vec_bf[4 * RT : 5 * RT, :], in_=log_in.rearrange("(r p) -> r p", p=P))
         for g in range(LP):
             load_dest(g, 0)
         load_base(2, 0, KC)
@@ -177,9 +174,7 @@ def tile_gravity_importation_scenarios_s1_kernel(
 
         def moving(g, lo, width):
             if g < BP:
-                i = 0 if g < SCALE_PARTS[0][1] else 1
-                words = w_words[:, g, 2 * lo : 2 * (lo + width)].bitcast(FP4X4)
-                return words, w_scales[i][:, g - SCALE_PARTS[i][0], lo : lo + width]
+                return w_words[:, g, 2 * lo : 2 * (lo + width)].bitcast(FP4X4), w_scales[:, g, lo : lo + width]
             return d_codes[:, g - BP, lo : lo + width].bitcast(FP8X4), d_scales[:, g - BP, lo : lo + width]
 
         def mm(r, n, g):
@@ -242,43 +237,48 @@ def tile_gravity_importation_scenarios_s1_kernel(
         turn(0, 0, direct=True)
         evac(0, 0)
         turn(1, 0, direct=True)
-        evac(1, 0)
         quant(0, 0, 1)
+        evac(1, 0)
         mm_part(0, 0)
-        permute(0, 2, BP)
         quant(1, 0, 1)
+        permute(0, 2, BP)
         turn(0, 1)
         turn(0, 2)
         mm_part(1, 0)
-        permute(1, 2, BP)
         evac(0, 1)
-        evac(0, 2, on_scalar=False)
+        permute(1, 2, BP)
+        evac(0, 2)
         quant(0, 1, 2)
         quant(0, 2, 3)
-        nc.vector.tensor_copy(out=vec_f32[:], in_=vec_bf[:])
-        permute(0, BP, PASSES)
-        permute(1, BP, PASSES)
         turn(1, 1)
         turn(1, 2)
-        vec_bank = psum.tile([P, 2, 2, P], F32, name="vec_bank", tag="bank6")
-        nc.tensor.transpose(vec_bank[:, 0, 0, :], vec_f32[:], ident[:])
         mm_part(0, 1)
         mm_part(0, 2)
         evac(1, 1)
+        permute(0, BP, PASSES)
         evac(1, 2, on_scalar=False)
-        nc.scalar.copy(out=cols[:], in_=vec_bank[:, 0, 0, 0 : 5 * RT])
+        permute(1, BP, PASSES)
         quant(1, 1, 2)
-        interleave(0, 0, 0, True)
-        interleave(0, 0, 1, False)
-        interleave(1, 0, 0, True)
-        interleave(1, 0, 1, False)
         quant(1, 2, 3)
-        quant_dest(0, 0)
+        interleave(0, 0, 0, False)
+        interleave(0, 0, 1, True)
+        nc.vector.tensor_copy(out=vec_f32[:], in_=vec_bf[:])
         for r in range(6, RT):
             load_base(r, 0, KC)
             load_live(r)
+        vec_bank = psum.tile([P, 2, 2, P], F32, name="vec_bank", tag="bank6")
+        nc.tensor.transpose(vec_bank[:, 0, 0, :], vec_f32[:], ident[:])
         turn(0, 3)
         turn(1, 3)
+        mm_part(1, 1)
+        mm_part(1, 2)
+        interleave(1, 0, 0, True)
+        nc.vector.tensor_copy(out=cols[:], in_=vec_bank[:, 0, 0, 0 : 5 * RT])
+        evac(0, 3, on_scalar=False)
+        interleave(1, 0, 1, False)
+        evac(1, 3, on_scalar=False)
+        quant_dest(0, 0)
+        permute(2, 0, PASSES)
         login_bank = []
         for n in range(2):
             bank = psum.tile([P, 4, P], F32, name="login_bank", tag=f"bank{6 + n}")
@@ -286,73 +286,44 @@ def tile_gravity_importation_scenarios_s1_kernel(
             for c in range(4):
                 col = 4 * RT + 4 * n + c
                 nc.tensor.transpose(bank[:, c, :], cols[:, col : col + 1].to_broadcast([P, P]), ident[:])
-        mm_part(1, 1)
-        mm_part(1, 2)
-        evac(0, 3)
-        evac(1, 3, on_scalar=False)
+        turn(2, 0)
+        turn(2, 1)
         for n in range(2):
             nc.scalar.copy(out=login[:, n * NT : (n + 1) * NT], in_=login_bank[n][:].rearrange("p c r -> p (c r)"))
+        turn(2, 2)
+        turn(2, 3)
         quant(0, 3, 4)
         quant_dest(1, 0)
-        permute(2, 0, BP)
         quant(1, 3, 4)
         mm_live(0)
         interleave(0, 1, 0, True)
         interleave(0, 1, 1, False)
-        interleave(1, 1, 0, True)
-        interleave(1, 1, 1, False)
-        permute(2, BP, PASSES)
-        for q in range(4):
-            turn(2, q)
+        interleave(1, 1, 0, False)
+        interleave(1, 1, 1, True)
         quant_dest(0, 1)
         evac(2, 0)
         add(0, 0)
-        evac(2, 1)
         quant_dest(1, 1)
+        evac(2, 1)
         mm_live(1)
         exp(0, 0)
-        add(1, 0)
         evac(2, 2)
-        quant(2, 0, 2)
-        exp(1, 0)
-        evac(2, 3, on_scalar=False)
-        add(0, 1)
-        quant(2, 2, 4)
         permute(3, 0, PASSES)
-        exp(0, 1)
+        evac(2, 3)
+        add(1, 0)
         mul(0, 0, 2)
-        add(1, 1)
+        add(0, 1)
+        exp(1, 0)
+        quant(2, 0, 2)
+        exp(0, 1)
+        quant(2, 2, 4)
         mul_v(0, 0)
-        mul(1, 0, 2)
-        for g in range(PASSES):
-            mm(2, 0, g)
-        for q in range(4):
-            turn(3, q)
-        for g in range(PASSES):
-            mm(2, 1, g)
-        exp(1, 1)
-        evac(3, 0)
-        permute(4, 0, PASSES)
-        evac(3, 1)
         mul(0, 1, 2)
-        add(2, 0)
-        evac(3, 2)
-        quant(3, 0, 2)
-        evac(3, 3)
         mul_v(0, 1)
         for z in range(3):
             store(0, z)
-        exp(2, 0)
-        mul_v(1, 0)
-        quant(3, 2, 4)
-        mul(1, 1, 2)
-        mul_v(1, 1)
-        for z in range(3):
-            store(1, z)
-        mul(2, 0, 2)
-        mul_v(2, 0)
 
-        for r in range(3, RT - 1):
+        for r in range(2, RT - 1):
             nxt = r + 1
             for q in range(4):
                 turn(nxt, q)
@@ -360,35 +331,42 @@ def tile_gravity_importation_scenarios_s1_kernel(
             for n in range(2):
                 for g in range(PASSES):
                     mm(r, n, g)
-            evac(nxt, 0)
+            for q in range(4):
+                evac(nxt, q)
+            mul_v(r - 1, 0)
             exp(r - 1, 1)
-            evac(nxt, 1)
+            mul(r - 1, 0, 2)
+            if r > HALVES_FROM:
+                for z in range(3):
+                    store_half(r - 1, 0, z)
             if r + 2 < RT:
                 permute(r + 2, 0, PASSES)
-            mul_v(r - 1, 1)
-            evac(nxt, 2)
             quant(nxt, 0, 2)
+            quant(nxt, 2, 4)
+            mul_v(r - 1, 1)
             mul(r - 1, 1, 2)
             for z in range(3):
-                store(r - 1, z)
-            evac(nxt, 3)
+                if r > HALVES_FROM:
+                    store_half(r - 1, 1, z)
+                else:
+                    store(r - 1, z)
             add(r, 0)
             exp(r, 0)
-            quant(nxt, 2, 4)
-            mul(r, 0, 2)
-            mul_v(r, 0)
 
         last = RT - 1
-        for z in range(3):
-            store_half(last - 1, 0, z)
         for g in range(PASSES):
             mm(last, 0, g)
+        mul(last - 1, 0, 2)
         add(last - 1, 1)
         exp(last - 1, 1)
-        mul_v(last - 1, 1)
+        mul_v(last - 1, 0)
+        for z in range(3):
+            store_half(last - 1, 0, z)
         mul(last - 1, 1, 2)
+        mul_v(last - 1, 1)
         for z in range(3):
             store_half(last - 1, 1, z)
+
         def last_add(i):
             lo, hi = LAST_CHUNKS[i]
             bank = psum.tile([P, NT], F32, name="acc", tag=f"bank{3 + i}")

@@ -23,7 +23,7 @@ BP = KC // 512
 LP = KL // 512
 PASSES = BP + LP
 HALVES_FROM = 4
-TURN_BANKS = ((4, 6, 7, 4), (5, 4, 5, 5))
+TURN_BANKS = ((4, 5, 6, 4), (0, 1, 2, 5))
 LAST_CHUNKS = ((0, 256), (256, 512))
 
 
@@ -47,10 +47,10 @@ def tile_gravity_importation_scenarios_s1_kernel(
         ]
         d_codes = keep.tile([P, LP, D], U32, name="d_codes", align_bytes=64)
         d_scales = keep.tile([P, LP, D], U8, name="d_scales", align_bytes=64)
-        login = keep.tile([P, D], F32, name="login", align_bytes=64)
+        login = keep.tile([P, D], BF16, name="login", align_bytes=64)
         vec_bf = keep.tile([P, P], BF16, name="vec_bf", align_bytes=64)
         vec_f32 = keep.tile([P, P], F32, name="vec_f32", align_bytes=64)
-        cols = keep.tile([P, 5 * RT], F32, name="cols", align_bytes=64)
+        cols = keep.tile([P, 4 * RT], F32, name="cols", align_bytes=64)
         junk = keep.tile([P, 8], F32, name="junk", align_bytes=64)
         raw = {}
 
@@ -87,24 +87,24 @@ def tile_gravity_importation_scenarios_s1_kernel(
             nc.sync.dma_start(out=d_raw[g][n][:], in_=dest_src[g][:, :, n * NT : (n + 1) * NT])
 
         load_base(0, 0, 1024)
+        load_base(0, 1024, KC)
         load_scales()
         load_base(1, 0, 1024)
-        load_words(0)
-        load_base(0, 1024, KC)
-        load_words(2)
         load_base(1, 1024, KC)
+        load_words(0)
+        load_words(2)
         load_words(4)
         load_live(0)
         load_live(1)
-        nc.gpsimd.dma_start(out=vec_bf[0:RT, :], in_=log_out.rearrange("(r p) -> r p", p=P))
-        nc.gpsimd.dma_start(out=vec_bf[RT : 4 * RT, :], in_=prevalence.rearrange("z (r p) -> (z r) p", p=P))
-        nc.gpsimd.dma_start(out=vec_bf[4 * RT : 5 * RT, :], in_=log_in.rearrange("(r p) -> r p", p=P))
+        nc.sync.dma_start(out=vec_bf[0:RT, :], in_=log_out.rearrange("(r p) -> r p", p=P))
+        nc.sync.dma_start(out=vec_bf[RT : 4 * RT, :], in_=prevalence.rearrange("z (r p) -> (z r) p", p=P))
         for g in range(LP):
             load_dest(g, 0)
         load_base(2, 0, KC)
         load_live(2)
         for g in range(LP):
             load_dest(g, 1)
+        nc.sync.dma_start(out=login[:], in_=log_in.partition_broadcast(P))
         for r in range(3, 6):
             load_base(r, 0, KC)
             load_live(r)
@@ -236,86 +236,72 @@ def tile_gravity_importation_scenarios_s1_kernel(
 
         turn(0, 0, direct=True)
         evac(0, 0)
-        turn(1, 0, direct=True)
-        quant(0, 0, 1)
-        evac(1, 0)
-        mm_part(0, 0)
-        quant(1, 0, 1)
         permute(0, 2, BP)
+        quant(0, 0, 1)
         turn(0, 1)
         turn(0, 2)
-        mm_part(1, 0)
+        permute(1, 0, 2)
         evac(0, 1)
-        permute(1, 2, BP)
         evac(0, 2)
-        quant(0, 1, 2)
-        quant(0, 2, 3)
+        turn(1, 0)
+        permute(1, 2, BP)
+        quant(0, 1, 3)
+        evac(1, 0)
+        quant(1, 0, 1)
         turn(1, 1)
         turn(1, 2)
-        mm_part(0, 1)
-        mm_part(0, 2)
         evac(1, 1)
+        evac(1, 2)
+        mm_part(0, 0)
+        mm_part(1, 0)
+        mm_part(0, 1)
+        quant(1, 1, 3)
+        mm_part(1, 1)
         permute(0, BP, PASSES)
-        evac(1, 2, on_scalar=False)
         permute(1, BP, PASSES)
-        quant(1, 1, 2)
-        quant(1, 2, 3)
-        interleave(0, 0, 0, False)
-        interleave(0, 0, 1, True)
         nc.vector.tensor_copy(out=vec_f32[:], in_=vec_bf[:])
         for r in range(6, RT):
             load_base(r, 0, KC)
             load_live(r)
-        vec_bank = psum.tile([P, 2, 2, P], F32, name="vec_bank", tag="bank6")
-        nc.tensor.transpose(vec_bank[:, 0, 0, :], vec_f32[:], ident[:])
         turn(0, 3)
         turn(1, 3)
-        mm_part(1, 1)
-        mm_part(1, 2)
-        interleave(1, 0, 0, True)
-        nc.vector.tensor_copy(out=cols[:], in_=vec_bank[:, 0, 0, 0 : 5 * RT])
-        evac(0, 3, on_scalar=False)
-        interleave(1, 0, 1, False)
-        evac(1, 3, on_scalar=False)
+        vec_bank = psum.tile([P, 2, 2, P], F32, name="vec_bank", tag="bank6")
+        nc.tensor.transpose(vec_bank[:, 0, 0, :], vec_f32[:], ident[:])
+        for r in range(2):
+            mm_part(r, 2)
+        interleave(0, 0, 0, False)
+        interleave(0, 0, 1, True)
+        interleave(1, 0, 0, False)
+        interleave(1, 0, 1, True)
         quant_dest(0, 0)
-        permute(2, 0, PASSES)
-        login_bank = []
-        for n in range(2):
-            bank = psum.tile([P, 4, P], F32, name="login_bank", tag=f"bank{6 + n}")
-            login_bank.append(bank)
-            for c in range(4):
-                col = 4 * RT + 4 * n + c
-                nc.tensor.transpose(bank[:, c, :], cols[:, col : col + 1].to_broadcast([P, P]), ident[:])
-        turn(2, 0)
-        turn(2, 1)
-        for n in range(2):
-            nc.scalar.copy(out=login[:, n * NT : (n + 1) * NT], in_=login_bank[n][:].rearrange("p c r -> p (c r)"))
-        turn(2, 2)
-        turn(2, 3)
+        nc.scalar.copy(out=cols[:], in_=vec_bank[:, 0, 0, 0 : 4 * RT])
+        evac(0, 3, on_scalar=False)
+        evac(1, 3)
         quant(0, 3, 4)
         quant_dest(1, 0)
-        quant(1, 3, 4)
-        mm_live(0)
         interleave(0, 1, 0, True)
         interleave(0, 1, 1, False)
+        quant(1, 3, 4)
+        for q in range(4):
+            turn(2, q, direct=True)
+        mm_live(0)
         interleave(1, 1, 0, False)
         interleave(1, 1, 1, True)
         quant_dest(0, 1)
-        evac(2, 0)
-        add(0, 0)
-        quant_dest(1, 1)
+        evac(2, 0, on_scalar=False)
         evac(2, 1)
-        mm_live(1)
-        exp(0, 0)
+        quant_dest(1, 1)
         evac(2, 2)
-        permute(3, 0, PASSES)
+        mm_live(1)
         evac(2, 3)
+        add(0, 0)
+        exp(0, 0)
         add(1, 0)
-        mul(0, 0, 2)
         add(0, 1)
         exp(1, 0)
         quant(2, 0, 2)
         exp(0, 1)
+        mul(0, 0, 2)
         quant(2, 2, 4)
         mul_v(0, 0)
         mul(0, 1, 2)
@@ -326,7 +312,7 @@ def tile_gravity_importation_scenarios_s1_kernel(
         for r in range(2, RT - 1):
             nxt = r + 1
             for q in range(4):
-                turn(nxt, q)
+                turn(nxt, q, direct=nxt == 3)
             add(r - 1, 1)
             for n in range(2):
                 for g in range(PASSES):

from contextlib import ExitStack

import concourse.mybir as mybir
from concourse.masks import make_identity

O, D, KL, KC, S = 1024, 1024, 1024, 3072, 3
FLOPS = 2 * O * D * (KL + KC)

F32 = mybir.dt.float32
BF16 = mybir.dt.bfloat16
I32 = mybir.dt.int32
U32 = mybir.dt.uint32
U8 = mybir.dt.uint8
FP8X4 = mybir.dt.float8_e4m3fn_x4
FP4X4 = mybir.dt.float4_e2m1fn_x4
ACT = mybir.ActivationFunctionType
ALU = mybir.AluOpType

P = 128
NT = 512
RT = O // P
BP = KC // 512
LP = KL // 512
PASSES = BP + LP
HALVES_FROM = 4
TURN_BANKS = ((4, 5, 6, 4), (0, 1, 2, 5))
LAST_CHUNKS = ((0, 256), (256, 512))


def tile_gravity_importation_scenarios_s1_kernel(
    tc, live, dest_live, base, catalogue_words, catalogue_scales, log_out, log_in, prevalence, out
):
    nc = tc.nc
    with ExitStack() as ctx:
        keep = ctx.enter_context(tc.tile_pool(name="keep", bufs=1))
        rawp = ctx.enter_context(tc.tile_pool(name="rawp", bufs=6))
        work = ctx.enter_context(tc.tile_pool(name="work", bufs=2))
        outp = ctx.enter_context(tc.tile_pool(name="outp", bufs=3))
        psum = ctx.enter_context(tc.psum_pool(name="psum", bufs=1))
        ctx.enter_context(tc.manual_schedule())

        ident = keep.tile([P, P], F32, name="ident", align_bytes=64)
        w_words = keep.tile([P, BP, 2 * D], U8, name="w_words", align_bytes=64)
        w_scales = keep.tile([P, BP, D], U8, name="w_scales", align_bytes=64)
        d_raw = [
            [keep.tile([P, 4, NT], BF16, name=f"d_raw{g}{n}", align_bytes=64) for n in range(2)] for g in range(LP)
        ]
        d_codes = keep.tile([P, LP, D], U32, name="d_codes", align_bytes=64)
        d_scales = keep.tile([P, LP, D], U8, name="d_scales", align_bytes=64)
        login = keep.tile([P, D], BF16, name="login", align_bytes=64)
        vec_bf = keep.tile([P, P], BF16, name="vec_bf", align_bytes=64)
        vec_f32 = keep.tile([P, P], F32, name="vec_f32", align_bytes=64)
        cols = keep.tile([P, 4 * RT], F32, name="cols", align_bytes=64)
        junk = keep.tile([P, 8], F32, name="junk", align_bytes=64)
        raw = {}

        scales_flat = w_scales[:].rearrange("p g n -> p (g n)").bitcast(I32)
        nc.vector.memset(scales_flat[:, 0:1024], 0)
        nc.gpsimd.memset(scales_flat[:, 1024:], 0)
        nc.vector.memset(vec_bf[:], 0.0)
        nc.vector.memset(junk[:], 0.0)
        make_identity(nc, ident[:])
        scales_src = catalogue_scales.bitcast(I32)
        nc.scalar.activation(out=junk[:, 0:1], in_=junk[:, 1:2], func=ACT.Exp)

        words_src = catalogue_words.bitcast(I32).rearrange("g p n -> p g n")
        words_dst = w_words[:].rearrange("p g n -> p (g n)").bitcast(I32).rearrange("p (g n) -> p g n", g=BP)
        dest_src = dest_live.rearrange("(g p j) n -> g p j n", g=LP, j=4)

        def load_scales():
            dst = scales_flat.rearrange("p (g n) -> p g n", g=BP)
            for q in range(4):
                nc.sync.dma_start(out=dst[q : P : 32, :, :], in_=scales_src[:, q : 16 : 4, :].rearrange("g r n -> r g n"))

        def load_base(r, a, b):
            if r not in raw:
                raw[r] = rawp.tile([P, KC + KL], BF16, name="raw", tag="raw", align_bytes=64)
            nc.sync.dma_start(out=raw[r][:, a:b], in_=base[r * P : (r + 1) * P, a:b])

        def load_live(r):
            nc.sync.dma_start(out=raw[r][:, KC:], in_=live[r * P : (r + 1) * P, :])

        def load_words(g):
            nc.sync.dma_start(out=words_dst[:, g : g + 2, :], in_=words_src[:, g : g + 2, :])

        def load_dest(g, n):
            nc.sync.dma_start(out=d_raw[g][n][:], in_=dest_src[g][:, :, n * NT : (n + 1) * NT])

        load_base(0, 0, 1024)
        load_base(0, 1024, KC)
        load_scales()
        load_base(1, 0, 1024)
        load_base(1, 1024, KC)
        load_words(0)
        load_words(2)
        load_words(4)
        load_live(0)
        load_live(1)
        nc.sync.dma_start(out=vec_bf[0:RT, :], in_=log_out.rearrange("(r p) -> r p", p=P))
        nc.sync.dma_start(out=vec_bf[RT : 4 * RT, :], in_=prevalence.rearrange("z (r p) -> (z r) p", p=P))
        for g in range(LP):
            load_dest(g, 0)
        load_base(2, 0, KC)
        load_live(2)
        for g in range(LP):
            load_dest(g, 1)
        nc.sync.dma_start(out=login[:], in_=log_in.partition_broadcast(P))
        for r in range(3, 6):
            load_base(r, 0, KC)
            load_live(r)

        perm, grp, codes, scales, tbank, acc, score, flow, res = {}, {}, {}, {}, {}, {}, {}, {}, {}

        def permute(r, a, b):
            if r not in perm:
                perm[r] = work.tile([P, (KC + KL) // 2], F32, name="perm", tag="perm", bufs=3, align_bytes=64)
            nc.vector.tensor_copy(
                out=perm[r][:, 256 * a : 256 * b].rearrange("q (g u p) -> q g u p", u=2, p=P),
                in_=raw[r][:].bitcast(F32)[:, 256 * a : 256 * b].rearrange("q (g p u) -> q g u p", u=2, p=P),
            )

        def turn(r, q, direct=False):
            b = 4 + q if r > 1 else TURN_BANKS[r][q]
            bank = psum.tile([P, 2, 2, P], F32, name="tbank", tag=f"bank{b}")
            tbank[r, q] = bank
            for a in range(2):
                g = 2 * q + a
                for u in range(2):
                    if direct:
                        src = raw[r][:].bitcast(F32)[:, 256 * g + u : 256 * (g + 1) : 2]
                    else:
                        src = perm[r][:, 256 * g + P * u : 256 * g + P * (u + 1)]
                    nc.tensor.transpose(bank[:, a, u, :], src, ident[:])

        def evac(r, q, on_scalar=True):
            if r not in grp:
                grp[r] = work.tile([P, PASSES * 512], BF16, name="grp", tag="grp", bufs=3, align_bytes=64)
            dst = grp[r][:, 1024 * q : 1024 * (q + 1)].bitcast(F32).rearrange("p (a r u) -> p a r u", a=2, u=2)
            src = tbank[r, q][:].rearrange("p a u r -> p a r u")
            if on_scalar:
                nc.scalar.copy(out=dst, in_=src)
            else:
                nc.vector.tensor_copy(out=dst, in_=src)

        def quant(r, a, b):
            if r not in codes:
                codes[r] = work.tile([P, PASSES * P], U32, name="codes", tag="codes", bufs=4, align_bytes=64)
                scales[r] = work.tile([P, PASSES * P], U8, name="scales", tag="scales", bufs=4, align_bytes=64)
            nc.vector.quantize_mx(
                out=codes[r][:, 256 * a : 256 * b].bitcast(FP8X4),
                scales=scales[r][:, 256 * a : 256 * b],
                in_=grp[r][:, 1024 * a : 1024 * b],
            )

        d_grp = {}

        def interleave(g, n, half, on_scalar):
            if (g, n) not in d_grp:
                d_grp[g, n] = work.tile([P, NT, 4], BF16, name="d_grp", tag="d_grp", align_bytes=64)
            part = slice(half * NT // 2, (half + 1) * NT // 2)
            dst = d_grp[g, n][:, part, :]
            src = d_raw[g][n][:, :, part].rearrange("p j n -> p n j")
            if on_scalar:
                nc.scalar.copy(out=dst, in_=src)
            else:
                nc.vector.tensor_copy(out=dst, in_=src)

        def quant_dest(g, n):
            nc.vector.quantize_mx(
                out=d_codes[:, g, n * NT : (n + 1) * NT].bitcast(FP8X4),
                scales=d_scales[:, g, n * NT : (n + 1) * NT],
                in_=d_grp[g, n][:].rearrange("p n j -> p (n j)"),
            )

        def moving(g, lo, width):
            if g < BP:
                return w_words[:, g, 2 * lo : 2 * (lo + width)].bitcast(FP4X4), w_scales[:, g, lo : lo + width]
            return d_codes[:, g - BP, lo : lo + width].bitcast(FP8X4), d_scales[:, g - BP, lo : lo + width]

        def mm(r, n, g):
            if g == 0:
                b = 2 * (r % 2) + n
                acc[r, n] = psum.tile([P, NT], F32, name="acc", tag=f"bank{b}")
            rhs, rhs_scale = moving(g, n * NT, NT)
            nc.tensor.matmul_mx(
                out=acc[r, n][:],
                lhsT=codes[r][:, g * P : (g + 1) * P].bitcast(FP8X4),
                lhsT_scale=scales[r][:, g * P : (g + 1) * P],
                rhs=rhs,
                rhs_scale=rhs_scale,
                start=(g == 0),
                stop=(g == PASSES - 1),
            )

        def add(r, n):
            score[r, n] = work.tile([P, NT], F32, name="score", tag="score", bufs=4, align_bytes=64)
            nc.vector.tensor_tensor(
                out=score[r, n][:], in0=acc[r, n][:], in1=login[:, n * NT : (n + 1) * NT], op=ALU.add
            )

        def exp(r, n):
            flow[r, n] = work.tile([P, NT], F32, name="flow", tag="flow", bufs=4, align_bytes=64)
            nc.scalar.activation(out=flow[r, n][:], in_=score[r, n][:], func=ACT.Exp, bias=cols[:, r : r + 1])

        def mul(r, n, z):
            if (r, z) not in res:
                res[r, z] = outp.tile([P, D], F32, name=f"res{z}", tag=f"res{z}", align_bytes=64)
            dst = res[r, z][:, n * NT : (n + 1) * NT]
            col = cols[:, (z + 1) * RT + r : (z + 1) * RT + r + 1]
            if z == 2:
                nc.scalar.activation(out=dst, in_=flow[r, n][:], func=ACT.Copy, scale=col)
            else:
                nc.vector.tensor_scalar(out=dst, in0=flow[r, n][:], scalar1=col, scalar2=None, op0=ALU.mult)

        def store(r, z):
            nc.sync.dma_start(out=out[z, r * P : (r + 1) * P, :], in_=res[r, z][:])

        def store_half(r, n, z):
            nc.sync.dma_start(
                out=out[z, r * P : (r + 1) * P, n * NT : (n + 1) * NT], in_=res[r, z][:, n * NT : (n + 1) * NT]
            )

        def mul_v(r, n):
            mul(r, n, 0)
            mul(r, n, 1)

        def mm_part(r, c):
            for g in (2 * c, 2 * c + 1):
                for n in range(2):
                    mm(r, n, g)

        def mm_live(n):
            for r in range(2):
                for g in range(BP, PASSES):
                    mm(r, n, g)

        turn(0, 0, direct=True)
        evac(0, 0)
        permute(0, 2, BP)
        quant(0, 0, 1)
        turn(0, 1)
        turn(0, 2)
        permute(1, 0, 2)
        evac(0, 1)
        evac(0, 2)
        turn(1, 0)
        permute(1, 2, BP)
        quant(0, 1, 3)
        evac(1, 0)
        quant(1, 0, 1)
        turn(1, 1)
        turn(1, 2)
        evac(1, 1)
        evac(1, 2)
        mm_part(0, 0)
        mm_part(1, 0)
        mm_part(0, 1)
        quant(1, 1, 3)
        mm_part(1, 1)
        permute(0, BP, PASSES)
        permute(1, BP, PASSES)
        nc.vector.tensor_copy(out=vec_f32[:], in_=vec_bf[:])
        for r in range(6, RT):
            load_base(r, 0, KC)
            load_live(r)
        turn(0, 3)
        turn(1, 3)
        vec_bank = psum.tile([P, 2, 2, P], F32, name="vec_bank", tag="bank6")
        nc.tensor.transpose(vec_bank[:, 0, 0, :], vec_f32[:], ident[:])
        for r in range(2):
            mm_part(r, 2)
        interleave(0, 0, 0, False)
        interleave(0, 0, 1, True)
        interleave(1, 0, 0, False)
        interleave(1, 0, 1, True)
        quant_dest(0, 0)
        nc.scalar.copy(out=cols[:], in_=vec_bank[:, 0, 0, 0 : 4 * RT])
        evac(0, 3, on_scalar=False)
        evac(1, 3)
        quant(0, 3, 4)
        quant_dest(1, 0)
        interleave(0, 1, 0, True)
        interleave(0, 1, 1, False)
        quant(1, 3, 4)
        for q in range(4):
            turn(2, q, direct=True)
        mm_live(0)
        interleave(1, 1, 0, False)
        interleave(1, 1, 1, True)
        quant_dest(0, 1)
        evac(2, 0, on_scalar=False)
        evac(2, 1)
        quant_dest(1, 1)
        evac(2, 2)
        mm_live(1)
        evac(2, 3)
        add(0, 0)
        exp(0, 0)
        add(1, 0)
        add(0, 1)
        exp(1, 0)
        quant(2, 0, 2)
        exp(0, 1)
        mul(0, 0, 2)
        quant(2, 2, 4)
        mul_v(0, 0)
        mul(0, 1, 2)
        mul_v(0, 1)
        for z in range(3):
            store(0, z)

        for r in range(2, RT - 1):
            nxt = r + 1
            for q in range(4):
                turn(nxt, q, direct=nxt == 3)
            add(r - 1, 1)
            for n in range(2):
                for g in range(PASSES):
                    mm(r, n, g)
            for q in range(4):
                evac(nxt, q)
            mul_v(r - 1, 0)
            exp(r - 1, 1)
            mul(r - 1, 0, 2)
            if r > HALVES_FROM:
                for z in range(3):
                    store_half(r - 1, 0, z)
            if r + 2 < RT:
                permute(r + 2, 0, PASSES)
            quant(nxt, 0, 2)
            quant(nxt, 2, 4)
            mul_v(r - 1, 1)
            mul(r - 1, 1, 2)
            for z in range(3):
                if r > HALVES_FROM:
                    store_half(r - 1, 1, z)
                else:
                    store(r - 1, z)
            add(r, 0)
            exp(r, 0)

        last = RT - 1
        for g in range(PASSES):
            mm(last, 0, g)
        mul(last - 1, 0, 2)
        add(last - 1, 1)
        exp(last - 1, 1)
        mul_v(last - 1, 0)
        for z in range(3):
            store_half(last - 1, 0, z)
        mul(last - 1, 1, 2)
        mul_v(last - 1, 1)
        for z in range(3):
            store_half(last - 1, 1, z)

        def last_add(i):
            lo, hi = LAST_CHUNKS[i]
            bank = psum.tile([P, NT], F32, name="acc", tag=f"bank{3 + i}")
            for c in range(lo, hi, P):
                for g in range(PASSES):
                    rhs, rhs_scale = moving(g, NT + c, P)
                    nc.tensor.matmul_mx(
                        out=bank[:, c - lo : c - lo + P],
                        lhsT=codes[last][:, g * P : (g + 1) * P].bitcast(FP8X4),
                        lhsT_scale=scales[last][:, g * P : (g + 1) * P],
                        rhs=rhs,
                        rhs_scale=rhs_scale,
                        start=(g == 0),
                        stop=(g == PASSES - 1),
                    )
            score[last, 1 + i] = work.tile([P, NT], F32, name="score", tag="score", bufs=4, align_bytes=64)
            nc.vector.tensor_tensor(
                out=score[last, 1 + i][:, : hi - lo],
                in0=bank[:, : hi - lo],
                in1=login[:, NT + lo : NT + hi],
                op=ALU.add,
            )

        def last_exp(i):
            w = LAST_CHUNKS[i][1] - LAST_CHUNKS[i][0]
            flow[last, 1 + i] = work.tile([P, NT], F32, name="flow", tag="flow", bufs=4, align_bytes=64)
            nc.scalar.activation(
                out=flow[last, 1 + i][:, :w],
                in_=score[last, 1 + i][:, :w],
                func=ACT.Exp,
                bias=cols[:, last : last + 1],
            )

        def last_mul(i):
            lo, hi = LAST_CHUNKS[i]
            for z in (0, 2, 1):
                col = cols[:, (z + 1) * RT + last : (z + 1) * RT + last + 1]
                dst = res[last, z][:, NT + lo : NT + hi]
                src = flow[last, 1 + i][:, : hi - lo]
                if z == 2:
                    nc.scalar.activation(out=dst, in_=src, func=ACT.Copy, scale=col)
                else:
                    nc.vector.tensor_scalar(out=dst, in0=src, scalar1=col, scalar2=None, op0=ALU.mult)
                nc.sync.dma_start(out=out[z, last * P : (last + 1) * P, NT + lo : NT + hi], in_=dst)

        add(last, 0)
        exp(last, 0)
        last_add(0)
        mul_v(last, 0)
        last_exp(0)
        mul(last, 0, 2)
        for z in range(3):
            store_half(last, 0, z)
        last_add(1)
        last_exp(1)
        last_mul(0)
        last_mul(1)
